import numpy as np
import ml_dtypes

BF16 = ml_dtypes.bfloat16


def bf(x):
    return np.asarray(x, np.float32).astype(BF16)


def f32(x):
    return np.asarray(x, np.float32)


def f64(x):
    return np.asarray(x).astype(np.float64)


def striped(idx):
    return np.concatenate([l.reshape(-1, 16).T for l in idx])


def rows(idx, k):
    return np.tile(np.repeat(idx, 16, axis=0), (k // (16 * 8), 1))


def look(tab, idx):
    return np.take_along_axis(f64(tab), rows(idx, len(tab)), axis=1)


K, S, V, N, M = 512, 2048, 1024, 1024, 256


def setup_inputs():
    return {"tab": bf(0.5 * np.random.standard_normal((K, S))), "y": f32(np.random.standard_normal((K, V))), "w": bf(np.random.standard_normal((K, M)) / np.sqrt(K)), "b": f32(0.5 * np.random.standard_normal((M, 1))), "offs": striped(np.stack([np.random.permutation(S)[:N] for _ in range(8)]))}


def reference(tab, y, w, b, offs):
    idx = np.stack([g.T.reshape(-1) for g in np.split(offs, 8)])
    t = look(tab, idx)
    x = np.exp(t) * f64(y)
    y = f64(w).T @ x
    return np.maximum(y + f64(b), 0.0)

@@ -1,0 +1,71 @@
+import concourse.mybir as mybir
+
+F32, BF16, U16 = mybir.dt.float32, mybir.dt.bfloat16, mybir.dt.uint16
+EXP = mybir.ActivationFunctionType.Exp
+ADD, MULT, MAX = mybir.AluOpType.add, mybir.AluOpType.mult, mybir.AluOpType.max
+
+P = 128
+PIECE = 512
+
+FLOPS = 2 * 512 * 256 * 1024
+
+
+def tile_lookup_gate_exp_relu_kernel(tc, tab, y, w, b, offs, out):
+    nc = tc.nc
+    rows, table_cols = tab.shape
+    n = y.shape[1]
+    m = w.shape[1]
+    row_blocks, out_blocks, pieces = rows // P, m // P, n // PIECE
+    piece_cols = PIECE // 16
+
+    with (
+        tc.tile_pool(name="held", bufs=1) as held,
+        tc.tile_pool(name="work", bufs=3) as work,
+        tc.psum_pool(name="psum", bufs=1) as psum,
+    ):
+        offsets = held.tile([P, n // 16], U16, name="offsets")
+        nc.sync.dma_start(offsets[:], offs)
+        windows = []
+        for r in range(row_blocks):
+            window = held.tile([P, table_cols], BF16, name=f"window{r}")
+            nc.sync.dma_start(window[:], tab[r * P : (r + 1) * P, :])
+            windows.append(window)
+        weights = held.tile([P, row_blocks, m], BF16, name="weights")
+        nc.sync.dma_start(weights[:], w.rearrange("(r p) m -> p r m", p=P))
+        streams = {}
+        for h in range(pieces):
+            for r in range(row_blocks):
+                stream = held.tile([P, PIECE], F32, name=f"stream{h}_{r}")
+                nc.sync.dma_start(stream[:], y[r * P : (r + 1) * P, h * PIECE : (h + 1) * PIECE])
+                streams[h, r] = stream
+        biases = []
+        for k in range(out_blocks):
+            bias = held.tile([P, 1], F32, name=f"bias{k}")
+            nc.gpsimd.dma_start(bias[:], b[k * P : (k + 1) * P, :])
+            biases.append(bias)
+
+        for h in range(pieces):
+            sums = [psum.tile([P, PIECE], F32, name=f"sum{h}_{k}") for k in range(out_blocks)]
+            for r in range(row_blocks):
+                gate = work.tile([P, PIECE], F32, name="gate")
+                nc.scalar.activation(
+                    gate[:],
+                    windows[r][:].indirect(offsets[:, h * piece_cols : (h + 1) * piece_cols]),
+                    EXP,
+                )
+                gated = work.tile([P, PIECE], BF16, name="gated")
+                nc.vector.tensor_tensor(gated[:], gate[:], streams[h, r][:], MULT)
+                for k in range(out_blocks):
+                    nc.tensor.matmul(
+                        sums[k][:],
+                        weights[:, r, k * P : (k + 1) * P],
+                        gated[:],
+                        start=r == 0,
+                        stop=r == row_blocks - 1,
+                    )
+            for k in range(out_blocks):
+                result = work.tile([P, PIECE], F32, name="result")
+                nc.vector.tensor_scalar(result[:], sums[k][:], biases[k][:], 0.0, ADD, MAX)
+                nc.sync.dma_start(
+                    out[k * P : (k + 1) * P, h * PIECE : (h + 1) * PIECE], result[:]
+                )

@@ -23,6 +23,11 @@ def tile_lookup_gate_exp_relu_kernel(tc, tab, y, w, b, offs, out):
         tc.tile_pool(name="work", bufs=3) as work,
         tc.psum_pool(name="psum", bufs=1) as psum,
     ):
+        zero = held.tile([P, 1], F32, name="zero")
+        one = held.tile([P, 1], F32, name="one")
+        nc.vector.memset(zero[:], 0.0)
+        nc.scalar.activation(one[:], zero[:], EXP)
+
         offsets = held.tile([P, n // 16], U16, name="offsets")
         nc.sync.dma_start(offsets[:], offs)
         windows = []

@@ -2,10 +2,12 @@ import concourse.mybir as mybir
 
 F32, BF16, U16 = mybir.dt.float32, mybir.dt.bfloat16, mybir.dt.uint16
 EXP = mybir.ActivationFunctionType.Exp
+RELU = mybir.ActivationFunctionType.Relu
 ADD, MULT, MAX = mybir.AluOpType.add, mybir.AluOpType.mult, mybir.AluOpType.max
 
 P = 128
 PIECE = 512
+HALF = 256
 
 FLOPS = 2 * 512 * 256 * 1024
 
@@ -20,7 +22,7 @@ def tile_lookup_gate_exp_relu_kernel(tc, tab, y, w, b, offs, out):
 
     with (
         tc.tile_pool(name="held", bufs=1) as held,
-        tc.tile_pool(name="work", bufs=3) as work,
+        tc.tile_pool(name="work", bufs=4) as work,
         tc.psum_pool(name="psum", bufs=1) as psum,
     ):
         zero = held.tile([P, 1], F32, name="zero")
@@ -49,28 +51,52 @@ def tile_lookup_gate_exp_relu_kernel(tc, tab, y, w, b, offs, out):
             nc.gpsimd.dma_start(bias[:], b[k * P : (k + 1) * P, :])
             biases.append(bias)
 
+        sums = {
+            (h, k, c): psum.tile([P, HALF], F32, name=f"sum{h}_{k}_{c}")
+            for h in range(pieces)
+            for k in range(out_blocks)
+            for c in range(0, PIECE, HALF)
+        }
+
+        def finish(h):
+            for k in range(out_blocks):
+                result = work.tile([P, PIECE], F32, name="result")
+                rows_out = out[k * P : (k + 1) * P, h * PIECE : (h + 1) * PIECE]
+                on_scalar = h == pieces - 1 and k % 2 == 0
+                for c in range(0, PIECE, HALF):
+                    half = result[:, c : c + HALF]
+                    if on_scalar:
+                        nc.scalar.activation(half, sums[h, k, c][:], RELU, bias=biases[k][:])
+                    else:
+                        nc.vector.tensor_scalar(
+                            half, sums[h, k, c][:], biases[k][:], 0.0, ADD, MAX
+                        )
+                if on_scalar:
+                    nc.scalar.dma_start(rows_out, result[:])
+                else:
+                    nc.sync.dma_start(rows_out, result[:])
+
         for h in range(pieces):
-            sums = [psum.tile([P, PIECE], F32, name=f"sum{h}_{k}") for k in range(out_blocks)]
             for r in range(row_blocks):
-                gate = work.tile([P, PIECE], F32, name="gate")
+                gate = held.tile([P, PIECE], F32, name=f"gate{r}")
                 nc.scalar.activation(
                     gate[:],
                     windows[r][:].indirect(offsets[:, h * piece_cols : (h + 1) * piece_cols]),
                     EXP,
                 )
-                gated = work.tile([P, PIECE], BF16, name="gated")
-                nc.vector.tensor_tensor(gated[:], gate[:], streams[h, r][:], MULT)
-                for k in range(out_blocks):
-                    nc.tensor.matmul(
-                        sums[k][:],
-                        weights[:, r, k * P : (k + 1) * P],
-                        gated[:],
-                        start=r == 0,
-                        stop=r == row_blocks - 1,
+                for c in range(0, PIECE, HALF):
+                    gated = work.tile([P, HALF], BF16, name="gated")
+                    nc.vector.tensor_tensor(
+                        gated[:], gate[:, c : c + HALF], streams[h, r][:, c : c + HALF], MULT
                     )
-            for k in range(out_blocks):
-                result = work.tile([P, PIECE], F32, name="result")
-                nc.vector.tensor_scalar(result[:], sums[k][:], biases[k][:], 0.0, ADD, MAX)
-                nc.sync.dma_start(
-                    out[k * P : (k + 1) * P, h * PIECE : (h + 1) * PIECE], result[:]
-                )
+                    for k in range(out_blocks):
+                        nc.tensor.matmul(
+                            sums[h, k, c][:],
+                            weights[:, r, k * P : (k + 1) * P],
+                            gated[:],
+                            start=r == 0,
+                            stop=r == row_blocks - 1,
+                        )
+                if h > 0 and r == row_blocks // 2 - 1:
+                    finish(h - 1)
+        finish(pieces - 1)

@@ -37,19 +37,36 @@ def tile_lookup_gate_exp_relu_kernel(tc, tab, y, w, b, offs, out):
             window = held.tile([P, table_cols], BF16, name=f"window{r}")
             nc.sync.dma_start(window[:], tab[r * P : (r + 1) * P, :])
             windows.append(window)
+
+        bias_rows = held.tile([32, m], F32, name="bias_rows")
+        nc.gpsimd.memset(bias_rows[:], 0.0)
+        nc.sync.dma_start(bias_rows[0:1, :], b.rearrange("m o -> o m"))
+        ones = held.tile([32, 1], F32, name="ones")
+        nc.gpsimd.memset(ones[:], 1.0)
+
         weights = held.tile([P, row_blocks, m], BF16, name="weights")
-        nc.sync.dma_start(weights[:], w.rearrange("(r p) m -> p r m", p=P))
         streams = {}
         for h in range(pieces):
             for r in range(row_blocks):
                 stream = held.tile([P, PIECE], F32, name=f"stream{h}_{r}")
                 nc.sync.dma_start(stream[:], y[r * P : (r + 1) * P, h * PIECE : (h + 1) * PIECE])
                 streams[h, r] = stream
-        biases = []
+                if h == 0 and r == 0:
+                    nc.sync.dma_start(weights[:], w.rearrange("(r p) m -> p r m", p=P))
+
+        bias_sums = psum.tile(
+            [P, out_blocks], F32, name="bias_sums", tag=f"sum{pieces - 1}_{out_blocks - 1}_{PIECE - HALF}"
+        )
         for k in range(out_blocks):
-            bias = held.tile([P, 1], F32, name=f"bias{k}")
-            nc.gpsimd.dma_start(bias[:], b[k * P : (k + 1) * P, :])
-            biases.append(bias)
+            nc.tensor.matmul(
+                bias_sums[:, k : k + 1],
+                bias_rows[:, k * P : (k + 1) * P],
+                ones[:],
+                start=True,
+                stop=True,
+            )
+        biases = held.tile([P, out_blocks], F32, name="biases")
+        nc.vector.tensor_copy(biases[:], bias_sums[:])
 
         sums = {
             (h, k, c): psum.tile([P, HALF], F32, name=f"sum{h}_{k}_{c}")
@@ -66,10 +83,10 @@ def tile_lookup_gate_exp_relu_kernel(tc, tab, y, w, b, offs, out):
                 for c in range(0, PIECE, HALF):
                     half = result[:, c : c + HALF]
                     if on_scalar:
-                        nc.scalar.activation(half, sums[h, k, c][:], RELU, bias=biases[k][:])
+                        nc.scalar.activation(half, sums[h, k, c][:], RELU, bias=biases[:, k : k + 1])
                     else:
                         nc.vector.tensor_scalar(
-                            half, sums[h, k, c][:], biases[k][:], 0.0, ADD, MAX
+                            half, sums[h, k, c][:], biases[:, k : k + 1], 0.0, ADD, MAX
                         )
                 if on_scalar:
                     nc.scalar.dma_start(rows_out, result[:])

import concourse.mybir as mybir

F32, BF16, U16 = mybir.dt.float32, mybir.dt.bfloat16, mybir.dt.uint16
EXP = mybir.ActivationFunctionType.Exp
RELU = mybir.ActivationFunctionType.Relu
ADD, MULT, MAX = mybir.AluOpType.add, mybir.AluOpType.mult, mybir.AluOpType.max

P = 128
PIECE = 512
HALF = 256

FLOPS = 2 * 512 * 256 * 1024


def tile_lookup_gate_exp_relu_kernel(tc, tab, y, w, b, offs, out):
    nc = tc.nc
    rows, table_cols = tab.shape
    n = y.shape[1]
    m = w.shape[1]
    row_blocks, out_blocks, pieces = rows // P, m // P, n // PIECE
    piece_cols = PIECE // 16

    with (
        tc.tile_pool(name="held", bufs=1) as held,
        tc.tile_pool(name="work", bufs=4) as work,
        tc.psum_pool(name="psum", bufs=1) as psum,
    ):
        zero = held.tile([P, 1], F32, name="zero")
        one = held.tile([P, 1], F32, name="one")
        nc.vector.memset(zero[:], 0.0)
        nc.scalar.activation(one[:], zero[:], EXP)

        offsets = held.tile([P, n // 16], U16, name="offsets")
        nc.sync.dma_start(offsets[:], offs)
        windows = []
        for r in range(row_blocks):
            window = held.tile([P, table_cols], BF16, name=f"window{r}")
            nc.sync.dma_start(window[:], tab[r * P : (r + 1) * P, :])
            windows.append(window)

        bias_rows = held.tile([32, m], F32, name="bias_rows")
        nc.gpsimd.memset(bias_rows[:], 0.0)
        nc.sync.dma_start(bias_rows[0:1, :], b.rearrange("m o -> o m"))
        ones = held.tile([32, 1], F32, name="ones")
        nc.gpsimd.memset(ones[:], 1.0)

        weights = held.tile([P, row_blocks, m], BF16, name="weights")
        streams = {}
        for h in range(pieces):
            for r in range(row_blocks):
                stream = held.tile([P, PIECE], F32, name=f"stream{h}_{r}")
                nc.sync.dma_start(stream[:], y[r * P : (r + 1) * P, h * PIECE : (h + 1) * PIECE])
                streams[h, r] = stream
                if h == 0 and r == 0:
                    nc.sync.dma_start(weights[:], w.rearrange("(r p) m -> p r m", p=P))

        bias_sums = psum.tile(
            [P, out_blocks], F32, name="bias_sums", tag=f"sum{pieces - 1}_{out_blocks - 1}_{PIECE - HALF}"
        )
        for k in range(out_blocks):
            nc.tensor.matmul(
                bias_sums[:, k : k + 1],
                bias_rows[:, k * P : (k + 1) * P],
                ones[:],
                start=True,
                stop=True,
            )
        biases = held.tile([P, out_blocks], F32, name="biases")
        nc.vector.tensor_copy(biases[:], bias_sums[:])

        sums = {
            (h, k, c): psum.tile([P, HALF], F32, name=f"sum{h}_{k}_{c}")
            for h in range(pieces)
            for k in range(out_blocks)
            for c in range(0, PIECE, HALF)
        }

        def finish(h):
            for k in range(out_blocks):
                result = work.tile([P, PIECE], F32, name="result")
                rows_out = out[k * P : (k + 1) * P, h * PIECE : (h + 1) * PIECE]
                on_scalar = h == pieces - 1 and k % 2 == 0
                for c in range(0, PIECE, HALF):
                    half = result[:, c : c + HALF]
                    if on_scalar:
                        nc.scalar.activation(half, sums[h, k, c][:], RELU, bias=biases[:, k : k + 1])
                    else:
                        nc.vector.tensor_scalar(
                            half, sums[h, k, c][:], biases[:, k : k + 1], 0.0, ADD, MAX
                        )
                if on_scalar:
                    nc.scalar.dma_start(rows_out, result[:])
                else:
                    nc.sync.dma_start(rows_out, result[:])

        for h in range(pieces):
            for r in range(row_blocks):
                gate = held.tile([P, PIECE], F32, name=f"gate{r}")
                nc.scalar.activation(
                    gate[:],
                    windows[r][:].indirect(offsets[:, h * piece_cols : (h + 1) * piece_cols]),
                    EXP,
                )
                for c in range(0, PIECE, HALF):
                    gated = work.tile([P, HALF], BF16, name="gated")
                    nc.vector.tensor_tensor(
                        gated[:], gate[:, c : c + HALF], streams[h, r][:, c : c + HALF], MULT
                    )
                    for k in range(out_blocks):
                        nc.tensor.matmul(
                            sums[h, k, c][:],
                            weights[:, r, k * P : (k + 1) * P],
                            gated[:],
                            start=r == 0,
                            stop=r == row_blocks - 1,
                        )
                if h > 0 and r == row_blocks // 2 - 1:
                    finish(h - 1)
        finish(pieces - 1)
